import numpy as np, ml_dtypes
CORES = [25,29,65,69,153,157,193,197]
N = 8
import mx_ref
BF = ml_dtypes.bfloat16
def entries(a):
    return np.ascontiguousarray(a.T).reshape(-1)
def table(e):
    return np.ascontiguousarray(np.reshape(e, (-1, 16)).T).astype(np.int32)
def gcols(t, e):
    v = np.concatenate([t.reshape(8, 16, -1, 4), np.zeros((8, 16, 1, 4), BF)], axis=2)
    return np.ascontiguousarray(np.stack([v[g][:, e[g]] for g in range(8)])).reshape(128, -1)
def cut(t, i, w=512):
    return t[:, w * i:w * i + w]
def f(rng, *shape):
    return mx_ref.flush((rng.standard_normal(shape, dtype=np.float32) * np.exp2(rng.integers(-2, 3, shape[:-1] + (1,)))).astype(BF))
def wide(rng, *shape, cols=0):
    v = rng.standard_normal(shape, dtype=np.float32) * np.exp2(rng.integers(-12, 13, shape)).astype(np.float32)
    if cols: v *= np.repeat(np.exp2(rng.integers(-cols, cols + 1, shape[:-2] + (1, shape[-1] // 4))) * (rng.random(shape[:-2] + (1, shape[-1] // 4)) > 0.0625), 4, axis=-1).astype(np.float32)
    return mx_ref.flush(v.astype(BF))
K, T, O = 256, 256, 3
SH = (7, 6, 5, 4, 3, 2, 1, 0)
A = (1531, 797, 1877, 1129, 619, 1993, 1367, 911)
B = (1013, 1741, 587, 1459, 1907, 733, 1229, 1667)
def levels(q):
    return list(range(8 // N * q, 8 // N * (q + 1)))
def owned(t):
    t = t.reshape(N, 8, 16, -1).copy()
    for q in range(N):
        for g in range(8):
            if g not in levels(q): t[q, g] = 0
    return t.reshape(N, 128, -1)
def pack(p):
    return np.stack([table(p[r]) for r in range(N)])
def places(rng):
    return {"px": pack(rng.integers(0, 1024, (N, T))), "py": pack(rng.integers(0, 1024, (N, T)))}
def setup_inputs(rng):
    return {"tb": owned(f(rng, N, 128, 4 * K)), **places(rng), "w": f(rng, N, 128, 512 * O)}
def setup_inputs_same(rng):
    d = setup_inputs(rng)
    d["px"] = pack(np.repeat(rng.integers(0, 1024, (N, 1)), T, axis=1)); d["py"] = pack(np.repeat(rng.integers(0, 1024, (N, 1)), T, axis=1))
    return d
def setup_inputs_corner(rng):
    d = setup_inputs(rng); c = rng.integers(0, 4, (N, T))
    for r in range(N): c[r, rng.permutation(T)[:4]] = np.arange(4)
    d["px"] = pack((c & 1) * 1023); d["py"] = pack((c >> 1) * 1023)
    return d
def setup_inputs_alike(rng):
    d = setup_inputs(rng)
    d["px"] = pack(np.repeat(rng.integers(0, 1024, (1, T)), N, axis=0)); d["py"] = pack(np.repeat(rng.integers(0, 1024, (1, T)), N, axis=0))
    return d
def setup_inputs_line(rng):
    d = setup_inputs(rng)
    d["px"] = pack(rng.integers(0, 1025 - T, (N, 1)) + np.arange(T)); d["py"] = pack(np.repeat(rng.integers(0, 1024, (N, 1)), T, axis=1))
    return d
def setup_inputs_spread(rng):
    d = setup_inputs(rng); d["tb"] = owned(wide(rng, N, 128, 4 * K, cols=4)); return d
def check_inputs(d):
    b = []
    for r in range(N):
        for n in ("px", "py"):
            e = entries(d[n][r])
            if e.min() < 0 or e.max() > 1023: b.append(n)
        t = d["tb"][r].reshape(8, 16, -1).astype(np.float32)
        if any((t[g] != 0).any() for g in range(8) if g not in levels(r)): b.append("tb")
    return b
def addresses(x, y):
    return np.stack([((x >> SH[g]) * A[g] + (y >> SH[g]) * B[g]) & (K - 1) for g in range(8)])
def reference(tb, px, py, w):
    y = np.zeros((N, 128, O * T), np.float32)
    for r in range(N):
        e = addresses(entries(px[r]), entries(py[r])); E = []
        for q in range(N):
            a = np.full((8, T), -1); a[levels(q)] = e[levels(q)]
            E.append(mx_ref.quantize(np.ascontiguousarray(gcols(tb[q], a))))
        for o in range(O):
            W = mx_ref.quantize(np.ascontiguousarray(cut(w[r], o)))
            Z = mx_ref.matmul(W, E[0])
            for q in range(1, N): Z = Z + mx_ref.matmul(W, E[q])
            y[r][:, T * o:T * o + T] = Z
    return {"y": y}

@@ -1,0 +1,291 @@
+from concourse.bass import DstId, RemoteDMATransfer
+from concourse.mybir import dt, AluOpType, ActivationFunctionType
+
+K, TOK, O, G = 256, 256, 3, 8
+SH = (7, 6, 5, 4, 3, 2, 1, 0)
+A = (1531, 797, 1877, 1129, 619, 1993, 1367, 911)
+B = (1013, 1741, 587, 1459, 1907, 733, 1229, 1667)
+SIDE = 1024
+JOINT = [l for l in range(G) if (SIDE >> SH[l]) ** 2 <= K]
+JSH = min(SH[l] for l in JOINT)
+JROW = SIDE >> JSH
+UNITS = [(tuple(JOINT), JSH, 1, JROW)] + [((l,), SH[l], A[l], B[l]) for l in range(G) if l not in JOINT]
+U = len(UNITS)
+C16 = TOK // 16
+H = K // 2
+BANKS = 8
+
+SCRATCH = {
+    "tbs": ("sbuf", [128, 4 * K], "bfloat16"), "tbg": ("sbuf", [128, 4 * K], "bfloat16"),
+    "qc": ("sbuf", [128, K], "float8_e4m3fn_x4"), "qp": ("sbuf", [128, K], "uint8"),
+    "wb": ("sbuf", [128, 512 * O], "bfloat16"),
+    "wc": ("sbuf", [128, 128 * O], "float8_e4m3fn_x4"), "wp": ("sbuf", [128, 128 * O], "uint8"),
+    "hc": ("sbuf", [128, H], "float8_e4m3fn_x4"), "hp": ("sbuf", [128, H], "uint8"),
+    "lc": ("sbuf", [128, G * K], "float8_e4m3fn_x4"), "lp": ("sbuf", [128, G * K], "uint8"),
+    "pxy": ("sbuf", [128, 2 * C16], "int32"), "mul": ("sbuf", [128, U * 2 * C16], "int32"),
+    "s1": ("sbuf", [128, U * 2 * C16], "int32"), "s2": ("sbuf", [128, U * 2 * C16], "int32"),
+    "s3": ("sbuf", [128, U * C16], "int32"), "s4": ("sbuf", [128, U * C16], "int32"),
+    "lst": ("sbuf", [128, U * C16], "uint16"),
+    "e0": ("sbuf", [128, 64], "int32"), "ex": ("sbuf", [128, 64], "int32"), "ey": ("sbuf", [128, 64], "int32"),
+    "et": ("sbuf", [128, 64], "int32"), "ex2": ("sbuf", [128, 64], "int32"), "ey2": ("sbuf", [128, 64], "int32"),
+    "es": ("sbuf", [128, 64], "int32"), "em": ("sbuf", [128, 64], "int32"), "ef": ("sbuf", [128, 64], "int32"),
+    "eo": ("sbuf", [128, 64], "uint16"),
+    "pick": ("sbuf", [128, U * O * K], "float32"), "acc": ("sbuf", [128, O * TOK], "float32"),
+    "ps": ("psum", [128, 512 * BANKS], "float32"),
+}
+SEMAPHORES = ["ldt", "ldw", "ldl", "v", "c", "m", "ix", "h", "loc", "sty"] + ["t%d" % q for q in range(G)]
+
+
+def bits(engines):
+    return sum(1 << e for e in engines)
+
+
+def direct(topo, src, ranks):
+    return [d for d in ranks if d != src and topo.may_write(src, d)]
+
+
+def far(topo, src, ranks):
+    return [d for d in ranks if d != src and not topo.may_write(src, d)]
+
+
+def far_near(topo, src, ranks):
+    return [d for d in far(topo, src, ranks) if topo.die(d) == topo.die(src)]
+
+
+def helpers(topo, src, ranks):
+    f = far(topo, src, ranks)
+    return [c for c in topo.cores_of(src) if c not in ranks and topo.die(c) == topo.die(src)
+            and all(topo.may_write(c, d) for d in f)][:2]
+
+
+def xfer(topo, core, dsts, engines, sem, src, outs):
+    ids = []
+    for d in dsts:
+        rid, pid = topo.addr(d, core)
+        ids.append(DstId(rid=rid, pnc=pid))
+    return RemoteDMATransfer(dst_ids=ids, dma_engine_mask=bits(engines), remote_sem=sem, srcs=[src], dsts=outs, alu_op=0)
+
+
+def helper_program(g, core, T, topo, ranks):
+    for r, src in enumerate(ranks):
+        hs = helpers(topo, src, ranks)
+        if core not in hs:
+            continue
+        h = hs.index(core)
+        dsts = far_near(topo, src, ranks)
+        eng = [e for e in topo.engines(core, dsts[0]) if all(e in topo.engines(core, d) for d in dsts)]
+        a, b = K * r + H * h, K * r + H * h + H
+        sem = T.sem["t%d" % r]
+        g.wait_ge(T.sem.h, 8)
+        g.remote_dma_fused([xfer(topo, core, dsts, eng, sem, T.hc[:].bitcast(dt.uint8),
+                                 [T.lc[:, a:b].bitcast(dt.uint8) for _ in dsts])], local_sem=T.sem.loc)
+        g.remote_dma_fused([xfer(topo, core, dsts, eng, sem, T.hp[:], [T.lp[:, a:b] for _ in dsts])], local_sem=T.sem.loc)
+        g.wait_ge(T.sem.loc, 2 * len(eng))
+
+
+def rank_program(g, core, T, topo):
+    ranks = list(T.cores)
+    rank = T.rank_of(core)
+    if rank is None:
+        helper_program(g, core, T, topo, ranks)
+        return
+    Op, AF = AluOpType, ActivationFunctionType
+    sem = T.sem
+    lvl = lambda q: sem["t%d" % q]
+
+    dirs = direct(topo, core, ranks)
+    mate = [d for d in dirs if d in topo.cores_of(core)][0]
+    plane = [d for d in dirs if d != mate]
+    hs = helpers(topo, core, ranks)
+    off = topo.engines(core, plane[0])
+    every = topo.engines(core, mate)
+    rest = [e for e in every if e not in off]
+    fwd = [q for q, c in enumerate(ranks) if core in far_near(topo, c, ranks)]
+
+    def kind(q):
+        c = ranks[q]
+        if c == core:
+            return 0
+        if c == mate:
+            return 1
+        if topo.may_write(c, core):
+            return 2
+        return 3 if q in fwd else 4
+
+    def expected(q):
+        k = kind(q)
+        if k == 1:
+            return 2 * len(rest)
+        if k == 2:
+            return 2 * len(off)
+        if k == 3:
+            return 4 * len(off)
+        return 2 * len(every)
+
+    units = sorted(UNITS, key=lambda u: max(kind(l) for l in u[0]))
+    seq = [(u, o) for u in range(U) for o in range(O)]
+    joint = rank in JOINT
+
+    g.sync.dma_start(T.tbs[:], T.tb[:]).then_inc(sem.ldt, 16)
+    g.sync.dma_start(T.wb[:], T.w[:]).then_inc(sem.ldw, 16)
+    n = 0
+    for i in range(8):
+        for t, name in enumerate(("px", "py")):
+            q = g.scalar if n % 4 != 3 else g.sync
+            q.dma_start(T.pxy[16 * i:16 * i + 16, C16 * t:C16 * t + C16], T[name][:]).then_inc(sem.ldl, 16)
+            n += 1
+
+    cmark, nc = {}, 0
+    plan = [("half",)] if joint else []
+    for u in range(U):
+        plan += [("cp", u, o) for o in range(O)]
+        if u == 1:
+            plan += [("ga", 0, O - 1)]
+    for x in plan:
+        nc += 1
+        cmark[x] = nc
+
+    vn = [0]
+
+    def v(inst):
+        inst.then_inc(sem.v, 1)
+        vn[0] += 1
+        return vn[0]
+
+    vec = g.vector
+    if joint:
+        g.iota(T.e0[:], [[16, 64]], -16 * rank, 1).then_inc(sem.ix, 1)
+        d = SH[rank] - JSH
+        lg = JROW.bit_length() - 1
+        vec.wait_ge(sem.ix, 1)
+        v(vec.tensor_scalar(T.ex[:], T.e0[:], 2 + d, (JROW >> d) - 1, Op.arith_shift_right, Op.bitwise_and))
+        v(vec.tensor_scalar(T.ey[:], T.e0[:], 2 + lg + d, (JROW >> d) - 1, Op.arith_shift_right, Op.bitwise_and))
+        m = v(vec.tensor_scalar(T.et[:], T.e0[:], 3, None, Op.bitwise_and))
+        vec.wait_ge(sem.v, m)
+        v(vec.tensor_scalar(T.ex2[:], T.ex[:], 4 * A[rank], None, Op.mult))
+        m = v(vec.tensor_scalar(T.ey2[:], T.ey[:], 4 * B[rank], None, Op.mult))
+        vec.wait_ge(sem.v, m)
+        m = v(vec.tensor_tensor(T.es[:], T.ex2[:], T.ey2[:], Op.add))
+        vec.wait_ge(sem.v, m)
+        m = v(vec.tensor_scalar(T.em[:], T.es[:], 4 * K - 1, None, Op.bitwise_and))
+        vec.wait_ge(sem.v, m)
+        m = v(vec.tensor_tensor(T.ef[:], T.em[:], T.et[:], Op.add))
+        vec.wait_ge(sem.v, m)
+        eo = v(vec.tensor_copy(T.eo[:], T.ef[:]))
+    for u, (_, _, a, b) in enumerate(units):
+        v(vec.memset(T.mul[:, 2 * C16 * u:2 * C16 * u + C16], a))
+        mulm = v(vec.memset(T.mul[:, 2 * C16 * u + C16:2 * C16 * u + 2 * C16], b))
+    vec.wait_ge(sem.ldt, 16)
+    tile = T.tbs
+    if joint:
+        vec.wait_ge(sem.v, eo)
+        m = v(vec.tensor_copy(T.tbg[:, 0:2 * K], T.tbs[:].indirect(T.eo[:, 0:32])))
+        vec.wait_ge(sem.v, m)
+        vec.wait_ge(sem.c, cmark[("half",)])
+        tile = T.tbg
+    qt = v(vec.quantize_mx(T.qc[:], T.qp[:], tile[:]))
+    vec.wait_ge(sem.ldw, 16)
+    qw = v(vec.quantize_mx(T.wc[:], T.wp[:], T.wb[:]))
+    vec.wait_ge(sem.ldl, 256)
+    for u, (_, sh, _, _) in enumerate(units):
+        s = slice(2 * C16 * u, 2 * C16 * u + 2 * C16)
+        m = v(vec.tensor_scalar(T.s1[:, s], T.pxy[:], sh, None, Op.arith_shift_right))
+    vec.wait_ge(sem.v, m)
+    m = v(vec.tensor_tensor(T.s2[:], T.s1[:], T.mul[:], Op.mult))
+    vec.wait_ge(sem.v, m)
+    for u in range(U):
+        a = 2 * C16 * u
+        m = v(vec.tensor_tensor(T.s3[:, C16 * u:C16 * u + C16], T.s2[:, a:a + C16], T.s2[:, a + C16:a + 2 * C16], Op.add))
+    vec.wait_ge(sem.v, m)
+    m = v(vec.tensor_scalar(T.s4[:], T.s3[:], K - 1, None, Op.bitwise_and))
+    vec.wait_ge(sem.v, m)
+    ml = v(vec.tensor_copy(T.lst[:], T.s4[:]))
+    vec.wait_ge(sem.v, ml)
+
+    def picked(u, o):
+        a = K * (O * u + o)
+        return T.pick[:, a:a + K].indirect(T.lst[:, C16 * u:C16 * u + C16])
+
+    last = [0] * O
+    for u, o in seq:
+        out = T.acc[:, TOK * o:TOK * o + TOK]
+        if u == 0:
+            if ("ga", u, o) in cmark:
+                continue
+            vec.wait_ge(sem.c, cmark[("cp", u, o)])
+            last[o] = v(vec.tensor_copy(out, picked(u, o)))
+            continue
+        need = cmark[("cp", u, o)]
+        if u == 1 and ("ga", 0, o) in cmark:
+            need = max(need, cmark[("ga", 0, o)])
+        vec.wait_ge(sem.c, need)
+        if last[o]:
+            vec.wait_ge(sem.v, last[o])
+        last[o] = v(vec.tensor_tensor(out, picked(u, o), out, Op.add))
+
+    total = 0
+    g.wait_ge(sem.v, qt)
+    half = len(rest) // 2
+    he = [rest[:half], rest[half:2 * half]]
+    g.remote_dma_fused([xfer(topo, core, [c], he[i], sem.h, T.qc[:, H * i:H * i + H].bitcast(dt.uint8),
+                             [T.hc[:].bitcast(dt.uint8)]) for i, c in enumerate(hs)], local_sem=sem.loc)
+    g.remote_dma_fused([xfer(topo, core, [c], he[i], sem.h, T.qp[:, H * i:H * i + H],
+                             [T.hp[:]]) for i, c in enumerate(hs)], local_sem=sem.loc)
+    total += 4 * half
+    s = slice(K * rank, K * rank + K)
+    g.remote_dma_fused([xfer(topo, core, d, e, lvl(rank), T.qc[:].bitcast(dt.uint8), [T.lc[:, s].bitcast(dt.uint8) for _ in d])
+                        for d, e in (([mate], rest), (plane, off))], local_sem=sem.loc)
+    g.remote_dma_fused([xfer(topo, core, d, e, lvl(rank), T.qp[:], [T.lp[:, s] for _ in d])
+                        for d, e in (([mate], rest), (plane, off))], local_sem=sem.loc)
+    total += 2 * (len(rest) + len(off))
+    rid, pid = topo.addr(mate, core)
+    for q in fwd:
+        s = slice(K * q, K * q + K)
+        g.wait_ge(lvl(q), expected(q))
+        g.remote_dma(T.lc[:, s].bitcast(dt.uint8), T.lc[:, s].bitcast(dt.uint8), lvl(q), sem.loc, pid, rid, bits(every))
+        g.remote_dma(T.lp[:, s], T.lp[:, s], lvl(q), sem.loc, pid, rid, bits(every))
+        total += 2 * len(every)
+    g.wait_ge(sem.loc, total)
+
+    pe = g.tensor
+    pe.wait_ge(sem.v, qw)
+    for u in range(U):
+        ls = sorted(units[u][0], key=kind)
+        for i, l in enumerate(ls):
+            if kind(l):
+                pe.wait_ge(lvl(l), expected(l))
+                co, sc = T.lc[:, K * l:K * l + K], T.lp[:, K * l:K * l + K]
+            else:
+                co, sc = T.qc[:], T.qp[:]
+            for o in range(O):
+                k = O * u + o
+                if i == 0 and k >= BANKS:
+                    pe.wait_ge(sem.c, cmark[("cp",) + seq[k - BANKS]])
+                b = 512 * (k % BANKS)
+                x = pe.matmul_mx(T.ps[:, b:b + K], T.wc[:, 128 * o:128 * o + 128], T.wp[:, 128 * o:128 * o + 128],
+                                 co, sc, i == 0, i == len(ls) - 1)
+                if i == len(ls) - 1:
+                    x.then_inc(sem.m, 1)
+
+    act = g.scalar
+    for x in plan:
+        if x[0] == "half":
+            act.wait_ge(sem.ldt, 16)
+            act.wait_ge(sem.v, eo)
+            y = act.activation(T.tbg[:, 2 * K:4 * K], T.tbs[:].indirect(T.eo[:, 32:64]), AF.Copy)
+        elif x[0] == "cp":
+            k = O * x[1] + x[2]
+            act.wait_ge(sem.m, k + 1)
+            b = 512 * (k % BANKS)
+            y = act.activation(T.pick[:, K * k:K * k + K], T.ps[:, b:b + K], AF.Copy)
+        else:
+            u, o = x[1], x[2]
+            act.wait_ge(sem.v, ml)
+            act.wait_ge(sem.c, cmark[("cp", u, o)])
+            y = act.activation(T.acc[:, TOK * o:TOK * o + TOK], picked(u, o), AF.Copy)
+        y.then_inc(sem.c, 1)
+
+    for o in range(O):
+        g.sync.wait_ge(sem.v, last[o])
+        g.sync.dma_start(T.y[:, TOK * o:TOK * o + TOK], T.acc[:, TOK * o:TOK * o + TOK]).then_inc(sem.sty, 16)
+    g.sync.wait_ge(sem.sty, 16 * O)

@@ -5,82 +5,87 @@ K, TOK, O, G = 256, 256, 3, 8
 SH = (7, 6, 5, 4, 3, 2, 1, 0)
 A = (1531, 797, 1877, 1129, 619, 1993, 1367, 911)
 B = (1013, 1741, 587, 1459, 1907, 733, 1229, 1667)
-SIDE = 1024
-JOINT = [l for l in range(G) if (SIDE >> SH[l]) ** 2 <= K]
-JSH = min(SH[l] for l in JOINT)
-JROW = SIDE >> JSH
-UNITS = [(tuple(JOINT), JSH, 1, JROW)] + [((l,), SH[l], A[l], B[l]) for l in range(G) if l not in JOINT]
-U = len(UNITS)
-C16 = TOK // 16
-H = K // 2
-BANKS = 8
+H = TOK // 2
+C = H // 16
+WB = 512 * O
+WC = 128 * O
 
 SCRATCH = {
-    "tbs": ("sbuf", [128, 4 * K], "bfloat16"), "tbg": ("sbuf", [128, 4 * K], "bfloat16"),
-    "qc": ("sbuf", [128, K], "float8_e4m3fn_x4"), "qp": ("sbuf", [128, K], "uint8"),
-    "wb": ("sbuf", [128, 512 * O], "bfloat16"),
-    "wc": ("sbuf", [128, 128 * O], "float8_e4m3fn_x4"), "wp": ("sbuf", [128, 128 * O], "uint8"),
+    "xy": ("sbuf", [128, 2 * C], "int32"), "mul": ("sbuf", [128, 8 * C], "int32"),
+    "s1": ("sbuf", [128, 8 * C], "int32"), "s2": ("sbuf", [128, 8 * C], "int32"),
+    "s3": ("sbuf", [128, 4 * C], "int32"), "s4": ("sbuf", [128, 4 * C], "int32"),
+    "lst": ("sbuf", [128, 4 * C], "uint16"), "hl": ("sbuf", [128, 2 * C], "uint16"), "nl": ("sbuf", [128, 4 * C], "uint16"),
+    "offf": ("sbuf", [128, 2 * C], "uint16"), "offn": ("sbuf", [128, 2 * C], "uint16"),
+    "tbs": ("sbuf", [128, 4 * K], "bfloat16"), "tbd": ("sbuf", [128, 4 * K], "bfloat16"),
+    "e": ("sbuf", [128, 16 * H], "bfloat16"),
+    "qc": ("sbuf", [128, 4 * H], "float8_e4m3fn_x4"), "qp": ("sbuf", [128, 4 * H], "uint8"),
+    "wz": ("sbuf", [128, 4 * WB], "bfloat16"),
+    "wc": ("sbuf", [128, 8 * WC], "float8_e4m3fn_x4"), "wp": ("sbuf", [128, 8 * WC], "uint8"),
     "hc": ("sbuf", [128, H], "float8_e4m3fn_x4"), "hp": ("sbuf", [128, H], "uint8"),
-    "lc": ("sbuf", [128, G * K], "float8_e4m3fn_x4"), "lp": ("sbuf", [128, G * K], "uint8"),
-    "pxy": ("sbuf", [128, 2 * C16], "int32"), "mul": ("sbuf", [128, U * 2 * C16], "int32"),
-    "s1": ("sbuf", [128, U * 2 * C16], "int32"), "s2": ("sbuf", [128, U * 2 * C16], "int32"),
-    "s3": ("sbuf", [128, U * C16], "int32"), "s4": ("sbuf", [128, U * C16], "int32"),
-    "lst": ("sbuf", [128, U * C16], "uint16"),
-    "e0": ("sbuf", [128, 64], "int32"), "ex": ("sbuf", [128, 64], "int32"), "ey": ("sbuf", [128, 64], "int32"),
-    "et": ("sbuf", [128, 64], "int32"), "ex2": ("sbuf", [128, 64], "int32"), "ey2": ("sbuf", [128, 64], "int32"),
-    "es": ("sbuf", [128, 64], "int32"), "em": ("sbuf", [128, 64], "int32"), "ef": ("sbuf", [128, 64], "int32"),
-    "eo": ("sbuf", [128, 64], "uint16"),
-    "pick": ("sbuf", [128, U * O * K], "float32"), "acc": ("sbuf", [128, O * TOK], "float32"),
-    "ps": ("psum", [128, 512 * BANKS], "float32"),
+    "lc": ("sbuf", [128, G * H], "float8_e4m3fn_x4"), "lp": ("sbuf", [128, G * H], "uint8"),
+    "acc": ("sbuf", [128, O * TOK], "float32"),
+    "ps": ("psum", [128, 512 * 2 * O], "float32"),
 }
-SEMAPHORES = ["ldt", "ldw", "ldl", "v", "c", "m", "ix", "h", "loc", "sty"] + ["t%d" % q for q in range(G)]
+SEMAPHORES = (["ldl", "ldt", "ln", "lf", "ix", "hl", "hcs", "hps", "v", "c", "m", "loc", "sty"]
+              + ["w%d" % s for s in range(4)] + ["t%d" % q for q in range(G)] + ["u%d" % q for q in range(G)])
 
 
 def bits(engines):
     return sum(1 << e for e in engines)
 
 
-def direct(topo, src, ranks):
-    return [d for d in ranks if d != src and topo.may_write(src, d)]
+def chips_of(topo, ranks):
+    out = []
+    for c in ranks:
+        if not any(c in p for p in out):
+            out.append([d for d in ranks if d in topo.cores_of(c)])
+    return out
 
 
-def far(topo, src, ranks):
-    return [d for d in ranks if d != src and not topo.may_write(src, d)]
-
-
-def far_near(topo, src, ranks):
-    return [d for d in far(topo, src, ranks) if topo.die(d) == topo.die(src)]
+def far_chips(topo, src, ranks):
+    return [p for p in chips_of(topo, ranks) if not topo.may_write(src, p[0])]
 
 
 def helpers(topo, src, ranks):
-    f = far(topo, src, ranks)
+    f = far_chips(topo, src, ranks)
     return [c for c in topo.cores_of(src) if c not in ranks and topo.die(c) == topo.die(src)
-            and all(topo.may_write(c, d) for d in f)][:2]
+            and all(topo.may_write(c, p[0]) for p in f)][:len(f)]
 
 
-def xfer(topo, core, dsts, engines, sem, src, outs):
+def slot(topo, core, ranks):
+    return [d for p in chips_of(topo, ranks) for d in p].index(core)
+
+
+def xfer(topo, core, dsts, engines, sem, src, out):
     ids = []
     for d in dsts:
         rid, pid = topo.addr(d, core)
         ids.append(DstId(rid=rid, pnc=pid))
-    return RemoteDMATransfer(dst_ids=ids, dma_engine_mask=bits(engines), remote_sem=sem, srcs=[src], dsts=outs, alu_op=0)
+    fold = isinstance(src, list)
+    return RemoteDMATransfer(dst_ids=ids, dma_engine_mask=bits(engines), remote_sem=sem, srcs=src if fold else [src],
+                             dsts=[out for _ in dsts], alu_op=1 if fold else 0)
 
 
 def helper_program(g, core, T, topo, ranks):
-    for r, src in enumerate(ranks):
+    for src in ranks:
         hs = helpers(topo, src, ranks)
         if core not in hs:
             continue
-        h = hs.index(core)
-        dsts = far_near(topo, src, ranks)
-        eng = [e for e in topo.engines(core, dsts[0]) if all(e in topo.engines(core, d) for d in dsts)]
-        a, b = K * r + H * h, K * r + H * h + H
-        sem = T.sem["t%d" % r]
-        g.wait_ge(T.sem.h, 8)
-        g.remote_dma_fused([xfer(topo, core, dsts, eng, sem, T.hc[:].bitcast(dt.uint8),
-                                 [T.lc[:, a:b].bitcast(dt.uint8) for _ in dsts])], local_sem=T.sem.loc)
-        g.remote_dma_fused([xfer(topo, core, dsts, eng, sem, T.hp[:], [T.lp[:, a:b] for _ in dsts])], local_sem=T.sem.loc)
-        g.wait_ge(T.sem.loc, 2 * len(eng))
+        pair = far_chips(topo, src, ranks)[hs.index(core)]
+        pair = sorted(pair, key=lambda d: topo.die(d) != topo.die(core))
+        eng = topo.engines(core, pair[0])
+        k = slot(topo, src, ranks)
+        sem, s = T.sem["t%d" % k], slice(H * k, H * k + H)
+        j = [src in p for p in far_chips(topo, pair[0], ranks)].index(True)
+        g.wait_ge(T.sem.hl, 16)
+        g.remote_dma_fused([xfer(topo, core, pair[:1], eng, T.sem.lf, [T.hl[:, 0:C], T.hl[:, C:2 * C]],
+                                 T.offf[:, C * j:C * j + C])], local_sem=T.sem.loc)
+        g.wait_ge(T.sem.hcs, 8)
+        g.remote_dma_fused([xfer(topo, core, pair[:1], eng, T.sem["u%d" % k], T.hc[:].bitcast(dt.uint8),
+                                 T.lc[:, s].bitcast(dt.uint8))], local_sem=T.sem.loc)
+        g.wait_ge(T.sem.hps, 8)
+        g.remote_dma_fused([xfer(topo, core, pair, eng, sem, T.hp[:], T.lp[:, s])], local_sem=T.sem.loc)
+        g.wait_ge(T.sem.loc, 3 * len(eng))
 
 
 def rank_program(g, core, T, topo):
@@ -90,202 +95,199 @@ def rank_program(g, core, T, topo):
         helper_program(g, core, T, topo, ranks)
         return
     Op, AF = AluOpType, ActivationFunctionType
-    sem = T.sem
-    lvl = lambda q: sem["t%d" % q]
+    sem, vec, act, pe, syn = T.sem, g.vector, g.scalar, g.tensor, g.sync
 
-    dirs = direct(topo, core, ranks)
-    mate = [d for d in dirs if d in topo.cores_of(core)][0]
-    plane = [d for d in dirs if d != mate]
+    chips = chips_of(topo, ranks)
+    fars = far_chips(topo, core, ranks)
+    home = [p for p in chips if core in p][0]
+    twin = [p for p in chips if p is not home and p not in fars][0]
+    tiles = fars + [home, twin]
+    sets = [home, twin] + fars
+    pos = home.index(core)
+    mate = home[1 - pos]
+    first, second = sorted(twin, key=lambda d: topo.die(d) != topo.die(core))
     hs = helpers(topo, core, ranks)
-    off = topo.engines(core, plane[0])
-    every = topo.engines(core, mate)
-    rest = [e for e in every if e not in off]
-    fwd = [q for q, c in enumerate(ranks) if core in far_near(topo, c, ranks)]
+    me = slot(topo, core, ranks)
+    off = topo.engines(core, first)
+    rest = [e for e in topo.engines(core, mate) if e not in off]
+    dead = slice(64 - 64 * pos, 128 - 64 * pos)
 
-    def kind(q):
-        c = ranks[q]
-        if c == core:
-            return 0
-        if c == mate:
-            return 1
-        if topo.may_write(c, core):
-            return 2
-        return 3 if q in fwd else 4
+    for t, (q, name) in enumerate(((syn, "px"), (act, "py"))):
+        for p in range(2):
+            for h in range(2):
+                a = 64 * p + 32 * pos + 16 * h
+                q.dma_start(T.xy[a:a + 16, C * t:C * t + C], T[name][:, C * h:C * h + C]).then_inc(sem.ldl, 16)
+    for k in range(4):
+        a = 64 * pos + 16 * k
+        syn.dma_start(T.tbs[a:a + 16, :], T.tb[16 * rank:16 * rank + 16, :]).then_inc(sem.ldt, 16)
+    z = 64 if rank < G // 2 else 0
+    syn.dma_start(T.tbs[dead, :], T.tb[z:z + 64, :]).then_inc(sem.ldt, 16)
 
-    def expected(q):
-        k = kind(q)
-        if k == 1:
-            return 2 * len(rest)
-        if k == 2:
-            return 2 * len(off)
-        if k == 3:
-            return 4 * len(off)
-        return 2 * len(every)
-
-    units = sorted(UNITS, key=lambda u: max(kind(l) for l in u[0]))
-    seq = [(u, o) for u in range(U) for o in range(O)]
-    joint = rank in JOINT
-
-    g.sync.dma_start(T.tbs[:], T.tb[:]).then_inc(sem.ldt, 16)
-    g.sync.dma_start(T.wb[:], T.w[:]).then_inc(sem.ldw, 16)
-    n = 0
-    for i in range(8):
-        for t, name in enumerate(("px", "py")):
-            q = g.scalar if n % 4 != 3 else g.sync
-            q.dma_start(T.pxy[16 * i:16 * i + 16, C16 * t:C16 * t + C16], T[name][:]).then_inc(sem.ldl, 16)
-            n += 1
-
-    cmark, nc = {}, 0
-    plan = [("half",)] if joint else []
-    for u in range(U):
-        plan += [("cp", u, o) for o in range(O)]
-        if u == 1:
-            plan += [("ga", 0, O - 1)]
-    for x in plan:
-        nc += 1
-        cmark[x] = nc
-
-    vn = [0]
+    vn, cn = [0], [0]
 
     def v(inst):
         inst.then_inc(sem.v, 1)
         vn[0] += 1
         return vn[0]
 
-    vec = g.vector
-    if joint:
-        g.iota(T.e0[:], [[16, 64]], -16 * rank, 1).then_inc(sem.ix, 1)
-        d = SH[rank] - JSH
-        lg = JROW.bit_length() - 1
-        vec.wait_ge(sem.ix, 1)
-        v(vec.tensor_scalar(T.ex[:], T.e0[:], 2 + d, (JROW >> d) - 1, Op.arith_shift_right, Op.bitwise_and))
-        v(vec.tensor_scalar(T.ey[:], T.e0[:], 2 + lg + d, (JROW >> d) - 1, Op.arith_shift_right, Op.bitwise_and))
-        m = v(vec.tensor_scalar(T.et[:], T.e0[:], 3, None, Op.bitwise_and))
-        vec.wait_ge(sem.v, m)
-        v(vec.tensor_scalar(T.ex2[:], T.ex[:], 4 * A[rank], None, Op.mult))
-        m = v(vec.tensor_scalar(T.ey2[:], T.ey[:], 4 * B[rank], None, Op.mult))
-        vec.wait_ge(sem.v, m)
-        m = v(vec.tensor_tensor(T.es[:], T.ex2[:], T.ey2[:], Op.add))
-        vec.wait_ge(sem.v, m)
-        m = v(vec.tensor_scalar(T.em[:], T.es[:], 4 * K - 1, None, Op.bitwise_and))
-        vec.wait_ge(sem.v, m)
-        m = v(vec.tensor_tensor(T.ef[:], T.em[:], T.et[:], Op.add))
-        vec.wait_ge(sem.v, m)
-        eo = v(vec.tensor_copy(T.eo[:], T.ef[:]))
-    for u, (_, _, a, b) in enumerate(units):
-        v(vec.memset(T.mul[:, 2 * C16 * u:2 * C16 * u + C16], a))
-        mulm = v(vec.memset(T.mul[:, 2 * C16 * u + C16:2 * C16 * u + 2 * C16], b))
-    vec.wait_ge(sem.ldt, 16)
-    tile = T.tbs
-    if joint:
-        vec.wait_ge(sem.v, eo)
-        m = v(vec.tensor_copy(T.tbg[:, 0:2 * K], T.tbs[:].indirect(T.eo[:, 0:32])))
-        vec.wait_ge(sem.v, m)
-        vec.wait_ge(sem.c, cmark[("half",)])
-        tile = T.tbg
-    qt = v(vec.quantize_mx(T.qc[:], T.qp[:], tile[:]))
-    vec.wait_ge(sem.ldw, 16)
-    qw = v(vec.quantize_mx(T.wc[:], T.wp[:], T.wb[:]))
-    vec.wait_ge(sem.ldl, 256)
-    for u, (_, sh, _, _) in enumerate(units):
-        s = slice(2 * C16 * u, 2 * C16 * u + 2 * C16)
-        m = v(vec.tensor_scalar(T.s1[:, s], T.pxy[:], sh, None, Op.arith_shift_right))
-    vec.wait_ge(sem.v, m)
-    m = v(vec.tensor_tensor(T.s2[:], T.s1[:], T.mul[:], Op.mult))
-    vec.wait_ge(sem.v, m)
-    for u in range(U):
-        a = 2 * C16 * u
-        m = v(vec.tensor_tensor(T.s3[:, C16 * u:C16 * u + C16], T.s2[:, a:a + C16], T.s2[:, a + C16:a + 2 * C16], Op.add))
-    vec.wait_ge(sem.v, m)
-    m = v(vec.tensor_scalar(T.s4[:], T.s3[:], K - 1, None, Op.bitwise_and))
-    vec.wait_ge(sem.v, m)
-    ml = v(vec.tensor_copy(T.lst[:], T.s4[:]))
-    vec.wait_ge(sem.v, ml)
+    def c(inst):
+        inst.then_inc(sem.c, 1)
+        cn[0] += 1
+        return cn[0]
 
-    def picked(u, o):
-        a = K * (O * u + o)
-        return T.pick[:, a:a + K].indirect(T.lst[:, C16 * u:C16 * u + C16])
+    for j, pair in enumerate(tiles):
+        for p, d in enumerate(pair):
+            l = T.rank_of(d)
+            g.iota(T.mul[64 * p:64 * p + 64, 2 * C * j:2 * C * j + 2 * C], [[B[l] - A[l], 2], [0, C]], A[l], 0).then_inc(sem.ix, 1)
 
-    last = [0] * O
-    for u, o in seq:
-        out = T.acc[:, TOK * o:TOK * o + TOK]
-        if u == 0:
-            if ("ga", u, o) in cmark:
-                continue
-            vec.wait_ge(sem.c, cmark[("cp", u, o)])
-            last[o] = v(vec.tensor_copy(out, picked(u, o)))
-            continue
-        need = cmark[("cp", u, o)]
-        if u == 1 and ("ga", 0, o) in cmark:
-            need = max(need, cmark[("ga", 0, o)])
-        vec.wait_ge(sem.c, need)
-        if last[o]:
-            vec.wait_ge(sem.v, last[o])
-        last[o] = v(vec.tensor_tensor(out, picked(u, o), out, Op.add))
+    def addresses(j):
+        w, n = slice(4 * C * j, 4 * C * j + 4 * C), slice(2 * C * j, 2 * C * j + 2 * C)
+        for i in (2 * j, 2 * j + 1):
+            for p, d in enumerate(tiles[i]):
+                r = slice(64 * p, 64 * p + 64)
+                m = v(vec.tensor_scalar(T.s1[r, 2 * C * i:2 * C * i + 2 * C], T.xy[r, :], SH[T.rank_of(d)], None,
+                                        Op.arith_shift_right))
+        vec.wait_ge(sem.v, m)
+        vec.wait_ge(sem.v, v(vec.tensor_tensor(T.s2[:, w], T.s1[:, w], T.mul[:, w], Op.mult)))
+        for i in (2 * j, 2 * j + 1):
+            a = 2 * C * i
+            m = v(vec.tensor_tensor(T.s3[:, C * i:C * i + C], T.s2[:, a:a + C], T.s2[:, a + C:a + 2 * C], Op.add))
+        vec.wait_ge(sem.v, m)
+        vec.wait_ge(sem.v, v(vec.tensor_scalar(T.s4[:, n], T.s3[:, n], K - 1, None, Op.bitwise_and)))
+        return v(vec.tensor_copy(T.lst[:, n], T.s4[:, n]))
 
-    total = 0
-    g.wait_ge(sem.v, qt)
-    half = len(rest) // 2
-    he = [rest[:half], rest[half:2 * half]]
-    g.remote_dma_fused([xfer(topo, core, [c], he[i], sem.h, T.qc[:, H * i:H * i + H].bitcast(dt.uint8),
-                             [T.hc[:].bitcast(dt.uint8)]) for i, c in enumerate(hs)], local_sem=sem.loc)
-    g.remote_dma_fused([xfer(topo, core, [c], he[i], sem.h, T.qp[:, H * i:H * i + H],
-                             [T.hp[:]]) for i, c in enumerate(hs)], local_sem=sem.loc)
-    total += 4 * half
-    s = slice(K * rank, K * rank + K)
-    g.remote_dma_fused([xfer(topo, core, d, e, lvl(rank), T.qc[:].bitcast(dt.uint8), [T.lc[:, s].bitcast(dt.uint8) for _ in d])
-                        for d, e in (([mate], rest), (plane, off))], local_sem=sem.loc)
-    g.remote_dma_fused([xfer(topo, core, d, e, lvl(rank), T.qp[:], [T.lp[:, s] for _ in d])
-                        for d, e in (([mate], rest), (plane, off))], local_sem=sem.loc)
-    total += 2 * (len(rest) + len(off))
-    rid, pid = topo.addr(mate, core)
-    for q in fwd:
-        s = slice(K * q, K * q + K)
-        g.wait_ge(lvl(q), expected(q))
-        g.remote_dma(T.lc[:, s].bitcast(dt.uint8), T.lc[:, s].bitcast(dt.uint8), lvl(q), sem.loc, pid, rid, bits(every))
-        g.remote_dma(T.lp[:, s], T.lp[:, s], lvl(q), sem.loc, pid, rid, bits(every))
-        total += 2 * len(every)
+    for p in range(2):
+        a = 64 * p + 32 - 32 * pos
+        v(vec.memset(T.xy[a:a + 32, :], 0))
+    v(vec.memset(T.offn[dead, :], 0))
+    z0 = v(vec.memset(T.wz[:, 0:WB], 0.0))
+    vec.wait_ge(sem.v, z0)
+    vec.wait_ge(sem.ldl, 128)
+    vec.wait_ge(sem.ix, 8)
+    afar = addresses(0)
+    anear = addresses(1)
+    z2 = v(vec.memset(T.wz[:, 2 * WB:4 * WB], 0.0))
+
+    act.wait_ge(sem.v, z0)
+    z1 = c(act.activation(T.wz[:, WB:2 * WB], T.wz[:, 0:WB], AF.Copy))
+    act.wait_ge(sem.ldt, 80)
+    for t in range(4):
+        apart = c(act.activation(T.tbd[:, K * t:K * t + K], T.tbs[:, t:4 * K:4], AF.Copy))
+    act.wait_ge(sem.c, apart)
+
+    def pick(j):
+        if j:
+            own, other = (slice(64 * pos + 32 * p, 64 * pos + 32 * p + 32) for p in (pos, 1 - pos))
+            vec.wait_ge(sem.v, anear)
+            v(vec.tensor_copy(T.offn[own, 0:C], T.lst[own, 2 * C:3 * C]))
+            vec.wait_ge(sem.ln, 16)
+            a, b = 2 * C * pos, 2 * C * (1 - pos)
+            v(vec.tensor_copy(T.offn[own, C:2 * C], T.nl[own, a + C:a + 2 * C]))
+            m = v(vec.tensor_copy(T.offn[other, :], T.nl[other, b:b + 2 * C]))
+            vec.wait_ge(sem.v, m)
+            act.wait_ge(sem.v, m)
+            vec.wait_ge(sem.c, apart)
+        else:
+            vec.wait_ge(sem.lf, 16)
+            act.wait_ge(sem.lf, 16)
+        a = 8 * H * j
+        for t in range(4):
+            out, win = T.e[:, a + t:a + 8 * H:4], T.tbd[:, K * t:K * t + K].indirect((T.offn if j else T.offf)[:])
+            if t < 2:
+                mv = v(vec.tensor_copy(out, win))
+            else:
+                mc = c(act.activation(out, win, AF.Copy))
+        vec.wait_ge(sem.v, mv)
+        vec.wait_ge(sem.c, mc)
+        s = slice(2 * H * j, 2 * H * j + 2 * H)
+        return v(vec.quantize_mx(T.qc[:, s], T.qp[:, s], T.e[:, a:a + 8 * H]))
+
+    def pack(i):
+        vec.wait_ge(sem["w%d" % i], 64)
+        for h in range(2):
+            a, b = WC * (2 * i + h), WB * (2 * (i % 2) + h)
+            m = v(vec.quantize_mx(T.wc[:, a:a + WC], T.wp[:, a:a + WC], T.wz[:, b:b + WB]))
+        return m
+
+    qnear = pick(1)
+    qfar = pick(0)
+    qw = [pack(i) for i in range(4)]
+
+    for i in range(4):
+        if i:
+            syn.wait_ge(sem.v, z2 if i == 1 else qw[i - 2])
+        else:
+            syn.wait_ge(sem.c, z1)
+        for h in range(2):
+            b = WB * (2 * (i % 2) + h)
+            for p, d in enumerate(sets[i]):
+                a, l = 64 * p + 16 * (2 * pos + h), T.rank_of(d)
+                syn.dma_start(T.wz[a:a + 16, b:b + WB], T.w[16 * l:16 * l + 16, :]).then_inc(sem["w%d" % i], 16)
+
+    g.wait_ge(sem.v, afar)
+    both = zip(hs, helpers(topo, mate, ranks))
+    g.remote_dma_fused([xfer(topo, core, list(d), e, sem.hl, T.lst[:, C * i:C * i + C], T.hl[:, C * pos:C * pos + C])
+                        for i, (d, e) in enumerate(zip(both, (off, rest)))], local_sem=sem.loc)
+    g.wait_ge(sem.v, anear)
+    a = 2 * C * pos
+    g.remote_dma_fused([xfer(topo, core, [d], e, sem.ln, T.lst[:, C * j:C * j + C], T.nl[:, a + C * (j - 2):a + C * (j - 1)])
+                        for d, j, e in ((first, 3, off[:4]), (second, 3, off[4:]), (mate, 2, rest))], local_sem=sem.loc)
+    total = 32
+    s, mysem = slice(H * me, H * me + H), sem["t%d" % me]
+
+    def send(ways, helper=False):
+        g.remote_dma_fused([xfer(topo, core, [d], e, sem.hcs if helper else mysem, T.qc[:, H * j:H * j + H].bitcast(dt.uint8),
+                                 (T.hc[:] if helper else T.lc[:, s]).bitcast(dt.uint8)) for d, j, e in ways], local_sem=sem.loc)
+        g.remote_dma_fused([xfer(topo, core, [d], e, sem.hps if helper else mysem, T.qp[:, H * j:H * j + H],
+                                 T.hp[:] if helper else T.lp[:, s]) for d, j, e in ways], local_sem=sem.loc)
+        return 2 * sum(len(e) for _, _, e in ways)
+
+    g.wait_ge(sem.v, qnear)
+    total += send([(first, 3, off), (mate, 2, rest)])
+    g.wait_ge(sem.v, qfar)
+    total += send([(hs[0], 0, off), (hs[1], 1, rest)], True)
+    early = [d for p in fars for d in p if topo.die(d) == topo.die(core)]
+    late = [d for p in fars for d in p if d not in early]
+    every = off + rest
+    for d in [first] + early:
+        k = slot(topo, d, ranks)
+        s, to = slice(H * k, H * k + H), sem["t%d" % k]
+        g.wait_ge(to if d == first else sem["u%d" % k], 16 if d == first else 8)
+        views = [T.lc[:, s].bitcast(dt.uint8)] + ([T.lp[:, s]] if d == first else [])
+        for x in views:
+            g.remote_dma_fused([xfer(topo, core, [mate], every, to, x, x)], local_sem=sem.loc)
+            total += len(every)
     g.wait_ge(sem.loc, total)
 
-    pe = g.tensor
-    pe.wait_ge(sem.v, qw)
-    for u in range(U):
-        ls = sorted(units[u][0], key=kind)
-        for i, l in enumerate(ls):
-            if kind(l):
-                pe.wait_ge(lvl(l), expected(l))
-                co, sc = T.lc[:, K * l:K * l + K], T.lp[:, K * l:K * l + K]
-            else:
-                co, sc = T.qc[:], T.qp[:]
-            for o in range(O):
-                k = O * u + o
-                if i == 0 and k >= BANKS:
-                    pe.wait_ge(sem.c, cmark[("cp",) + seq[k - BANKS]])
-                b = 512 * (k % BANKS)
-                x = pe.matmul_mx(T.ps[:, b:b + K], T.wc[:, 128 * o:128 * o + 128], T.wp[:, 128 * o:128 * o + 128],
-                                 co, sc, i == 0, i == len(ls) - 1)
-                if i == len(ls) - 1:
+    steps = [core, mate, first, second] + early + late
+    seen = qnear
+    pe.wait_ge(sem.v, seen)
+    for d in steps:
+        i = [j for j, p in enumerate(sets) if d in p][0]
+        if qw[i] > seen:
+            seen = qw[i]
+            pe.wait_ge(sem.v, seen)
+        k = slot(topo, d, ranks)
+        if d in early:
+            pe.wait_ge(sem["u%d" % k], 8)
+        if d != core:
+            pe.wait_ge(sem["t%d" % k], 8 if d in early else 24 if d in late else 32 if d == second else 16)
+        co, sc = (T.qc[:, 2 * H:3 * H], T.qp[:, 2 * H:3 * H]) if d == core else \
+            (T.lc[:, H * k:H * k + H], T.lp[:, H * k:H * k + H])
+        for o in range(O):
+            for h in range(2):
+                a, b = WC * (2 * i + h) + 128 * o, 512 * (2 * o + h)
+                x = pe.matmul_mx(T.ps[:, b:b + H], T.wc[:, a:a + 128], T.wp[:, a:a + 128], co, sc, d == core, d == steps[-1])
+                if d == steps[-1]:
                     x.then_inc(sem.m, 1)
 
-    act = g.scalar
-    for x in plan:
-        if x[0] == "half":
-            act.wait_ge(sem.ldt, 16)
-            act.wait_ge(sem.v, eo)
-            y = act.activation(T.tbg[:, 2 * K:4 * K], T.tbs[:].indirect(T.eo[:, 32:64]), AF.Copy)
-        elif x[0] == "cp":
-            k = O * x[1] + x[2]
-            act.wait_ge(sem.m, k + 1)
-            b = 512 * (k % BANKS)
-            y = act.activation(T.pick[:, K * k:K * k + K], T.ps[:, b:b + K], AF.Copy)
-        else:
-            u, o = x[1], x[2]
-            act.wait_ge(sem.v, ml)
-            act.wait_ge(sem.c, cmark[("cp", u, o)])
-            y = act.activation(T.acc[:, TOK * o:TOK * o + TOK], picked(u, o), AF.Copy)
-        y.then_inc(sem.c, 1)
-
     for o in range(O):
-        g.sync.wait_ge(sem.v, last[o])
-        g.sync.dma_start(T.y[:, TOK * o:TOK * o + TOK], T.acc[:, TOK * o:TOK * o + TOK]).then_inc(sem.sty, 16)
-    g.sync.wait_ge(sem.sty, 16 * O)
+        a, b = TOK * o, 512 * 2 * o
+        vec.wait_ge(sem.m, 2 * o + 1)
+        mv = v(vec.tensor_copy(T.acc[:, a:a + H], T.ps[:, b:b + H]))
+        act.wait_ge(sem.m, 2 * o + 2)
+        mc = c(act.activation(T.acc[:, a + H:a + TOK], T.ps[:, b + 512:b + 512 + H], AF.Copy))
+        syn.wait_ge(sem.v, mv)
+        syn.wait_ge(sem.c, mc)
+        syn.dma_start(T.y[:, a:a + TOK], T.acc[:, a:a + TOK]).then_inc(sem.sty, 16)
+    syn.wait_ge(sem.sty, 16 * O)

@@ -9,12 +9,17 @@ H = TOK // 2
 C = H // 16
 WB = 512 * O
 WC = 128 * O
+FAR0, FAR1, TWIN, HOME = range(4)
+
+PLAN = ([("lists", FAR0, 3), ("zero", 2), ("zero", 3), ("home",), ("pick", HOME, 2), ("pick", TWIN, 2),
+         ("codes", TWIN, 2), ("pick", FAR0, 2), ("codes", FAR0, 1), ("pick", FAR1, 2), ("codes", FAR1, 1)]
+        + [("pack", n) for n in range(8)])
 
 SCRATCH = {
-    "xy": ("sbuf", [128, 2 * C], "int32"), "mul": ("sbuf", [128, 8 * C], "int32"),
+    "xy": ("sbuf", [128, 2 * C], "int32"), "xm": ("sbuf", [128, 2 * C], "int32"), "mul": ("sbuf", [128, 8 * C], "int32"),
     "s1": ("sbuf", [128, 8 * C], "int32"), "s2": ("sbuf", [128, 8 * C], "int32"),
     "s3": ("sbuf", [128, 4 * C], "int32"), "s4": ("sbuf", [128, 4 * C], "int32"),
-    "lst": ("sbuf", [128, 4 * C], "uint16"), "hl": ("sbuf", [128, 2 * C], "uint16"), "nl": ("sbuf", [128, 4 * C], "uint16"),
+    "lst": ("sbuf", [128, 4 * C], "uint16"), "hl": ("sbuf", [128, 2 * C], "uint16"), "nl": ("sbuf", [128, 2 * C], "uint16"),
     "offf": ("sbuf", [128, 2 * C], "uint16"), "offn": ("sbuf", [128, 2 * C], "uint16"),
     "tbs": ("sbuf", [128, 4 * K], "bfloat16"), "tbd": ("sbuf", [128, 4 * K], "bfloat16"),
     "e": ("sbuf", [128, 16 * H], "bfloat16"),
@@ -26,8 +31,8 @@ SCRATCH = {
     "acc": ("sbuf", [128, O * TOK], "float32"),
     "ps": ("psum", [128, 512 * 2 * O], "float32"),
 }
-SEMAPHORES = (["ldl", "ldt", "ln", "lf", "ix", "hl", "hcs", "hps", "v", "c", "m", "loc", "sty"]
-              + ["w%d" % s for s in range(4)] + ["t%d" % q for q in range(G)] + ["u%d" % q for q in range(G)])
+SEMAPHORES = (["ldl", "ldt", "ldd", "ldz", "lm", "ln", "lf0", "lf1", "ix", "hl", "hcs", "hps", "v", "c", "m", "loc", "sty"]
+              + ["w%d" % s for s in range(8)] + ["t%d" % q for q in range(G)] + ["u%d" % q for q in range(G)])
 
 
 def bits(engines):
@@ -43,7 +48,8 @@ def chips_of(topo, ranks):
 
 
 def far_chips(topo, src, ranks):
-    return [p for p in chips_of(topo, ranks) if not topo.may_write(src, p[0])]
+    f = [p for p in chips_of(topo, ranks) if not topo.may_write(src, p[0])]
+    return sorted(f, key=lambda p: topo.host(p[0]) != topo.host(src))
 
 
 def helpers(topo, src, ranks):
@@ -78,12 +84,12 @@ def helper_program(g, core, T, topo, ranks):
         sem, s = T.sem["t%d" % k], slice(H * k, H * k + H)
         j = [src in p for p in far_chips(topo, pair[0], ranks)].index(True)
         g.wait_ge(T.sem.hl, 16)
-        g.remote_dma_fused([xfer(topo, core, pair[:1], eng, T.sem.lf, [T.hl[:, 0:C], T.hl[:, C:2 * C]],
+        g.remote_dma_fused([xfer(topo, core, pair[:1], eng, T.sem["lf%d" % j], [T.hl[:, 0:C], T.hl[:, C:2 * C]],
                                  T.offf[:, C * j:C * j + C])], local_sem=T.sem.loc)
-        g.wait_ge(T.sem.hcs, 8)
+        g.wait_ge(T.sem.hcs, 16)
         g.remote_dma_fused([xfer(topo, core, pair[:1], eng, T.sem["u%d" % k], T.hc[:].bitcast(dt.uint8),
                                  T.lc[:, s].bitcast(dt.uint8))], local_sem=T.sem.loc)
-        g.wait_ge(T.sem.hps, 8)
+        g.wait_ge(T.sem.hps, 16)
         g.remote_dma_fused([xfer(topo, core, pair, eng, sem, T.hp[:], T.lp[:, s])], local_sem=T.sem.loc)
         g.wait_ge(T.sem.loc, 3 * len(eng))
 
@@ -101,7 +107,7 @@ def rank_program(g, core, T, topo):
     fars = far_chips(topo, core, ranks)
     home = [p for p in chips if core in p][0]
     twin = [p for p in chips if p is not home and p not in fars][0]
-    tiles = fars + [home, twin]
+    tiles = fars + [twin, home]
     sets = [home, twin] + fars
     pos = home.index(core)
     mate = home[1 - pos]
@@ -110,18 +116,19 @@ def rank_program(g, core, T, topo):
     me = slot(topo, core, ranks)
     off = topo.engines(core, first)
     rest = [e for e in topo.engines(core, mate) if e not in off]
-    dead = slice(64 - 64 * pos, 128 - 64 * pos)
+    every = off + rest
+    live, dead = slice(64 * pos, 64 * pos + 64), slice(64 - 64 * pos, 128 - 64 * pos)
+    own, other = (slice(64 * pos + 32 * p, 64 * pos + 32 * p + 32) for p in (pos, 1 - pos))
 
     for t, (q, name) in enumerate(((syn, "px"), (act, "py"))):
-        for p in range(2):
-            for h in range(2):
-                a = 64 * p + 32 * pos + 16 * h
-                q.dma_start(T.xy[a:a + 16, C * t:C * t + C], T[name][:, C * h:C * h + C]).then_inc(sem.ldl, 16)
+        for h in range(2):
+            a = 32 * pos + 16 * h
+            q.dma_start(T.xy[a:a + 16, C * t:C * t + C], T[name][:, C * h:C * h + C]).then_inc(sem.ldl, 16)
     for k in range(4):
         a = 64 * pos + 16 * k
         syn.dma_start(T.tbs[a:a + 16, :], T.tb[16 * rank:16 * rank + 16, :]).then_inc(sem.ldt, 16)
     z = 64 if rank < G // 2 else 0
-    syn.dma_start(T.tbs[dead, :], T.tb[z:z + 64, :]).then_inc(sem.ldt, 16)
+    syn.dma_start(T.tbd[dead, :], T.tb[z:z + 64, :]).then_inc(sem.ldd, 16)
 
     vn, cn = [0], [0]
 
@@ -135,120 +142,132 @@ def rank_program(g, core, T, topo):
         cn[0] += 1
         return cn[0]
 
-    for j, pair in enumerate(tiles):
-        for p, d in enumerate(pair):
-            l = T.rank_of(d)
+    def addresses(j, n, parts, r, out):
+        w, u = slice(2 * C * j, 2 * C * (j + n)), slice(C * j, C * (j + n))
+        for i, rows, xy, d in parts:
+            m = v(vec.tensor_scalar(T.s1[rows, 2 * C * i:2 * C * i + 2 * C], xy, SH[T.rank_of(d)], None, Op.arith_shift_right))
+        vec.wait_ge(sem.ix, 7 if j == HOME else 2 * (j + n))
+        vec.wait_ge(sem.v, m)
+        vec.wait_ge(sem.v, v(vec.tensor_tensor(T.s2[r, w], T.s1[r, w], T.mul[r, w], Op.mult)))
+        for i in range(j, j + n):
+            a = 2 * C * i
+            m = v(vec.tensor_tensor(T.s3[r, C * i:C * i + C], T.s2[r, a:a + C], T.s2[r, a + C:a + 2 * C], Op.add))
+        vec.wait_ge(sem.v, m)
+        vec.wait_ge(sem.v, v(vec.tensor_scalar(T.s4[r, u], T.s3[r, u], K - 1, None, Op.bitwise_and)))
+        return v(vec.tensor_copy(out, T.s4[r, u]))
+
+    half = WB // 2
+    v(vec.memset(T.xy[32 - 32 * pos:64 - 32 * pos, :], 0))
+    blank = v(vec.memset(T.xy[64:128, :], 0))
+    v(vec.memset(T.offn[dead, :], 0))
+    zero = {0: v(vec.memset(T.wz[:, 0:WB], 0.0))}
+    seed = v(vec.memset(T.wz[:, 2 * WB:2 * WB + half], 0.0))
+    vec.wait_ge(sem.v, zero[0])
+    vec.wait_ge(sem.ldl, 64)
+
+    act.wait_ge(sem.ldt, 64)
+    for t in range(4):
+        apart = c(act.activation(T.tbd[live, K * t:K * t + K], T.tbs[live, t:4 * K:4], AF.Copy))
+    act.wait_ge(sem.v, seed)
+    copied = c(act.activation(T.wz[:, 3 * WB:3 * WB + half], T.wz[:, 2 * WB:2 * WB + half], AF.Copy))
+    act.wait_ge(sem.c, apart)
+    act.wait_ge(sem.ldd, 16)
+
+    lists, codes, packed = {}, {}, {}
+    for step in PLAN:
+        if step[0] == "lists":
+            j, n = step[1:]
+            parts = [(i, slice(64 * p, 64 * p + 64), T.xy[0:64, :], d) for i in range(j, j + n) for p, d in enumerate(tiles[i])]
+            lists[j] = addresses(j, n, parts, slice(0, 128), T.lst[:, C * j:C * (j + n)])
+        elif step[0] == "zero":
+            n = step[1]
+            zero[n] = v(vec.memset(T.wz[:, WB * n + half:WB * n + WB], 0.0))
+        elif step[0] == "home":
+            vec.wait_ge(sem.lm, 16)
+            lists[HOME] = addresses(HOME, 1, [(HOME, own, T.xy[32 * pos:32 * pos + 32, :], core),
+                                              (HOME, other, T.xm[32 - 32 * pos:64 - 32 * pos, :], core)],
+                                    live, T.offn[live, C:2 * C])
+            vec.wait_ge(sem.c, apart)
+            vec.wait_ge(sem.ldd, 16)
+        elif step[0] == "pick":
+            j, share = step[1:]
+            if j == TWIN:
+                vec.wait_ge(sem.ln, 8)
+                for r, p in ((own, pos), (other, 1 - pos)):
+                    m = v(vec.tensor_copy(T.offn[r, 0:C], T.nl[r, C * p:C * p + C]))
+            for q in (vec, act):
+                if j < TWIN:
+                    q.wait_ge(sem["lf%d" % j], 8)
+                else:
+                    q.wait_ge(sem.v, m if j == TWIN else lists[HOME])
+            offsets = T.offf[:, C * j:C * j + C] if j < TWIN else T.offn[:, C * (j - TWIN):C * (j - TWIN) + C]
+            for t in range(4):
+                out, win = T.e[:, 4 * H * j + t:4 * H * (j + 1):4], T.tbd[:, K * t:K * t + K].indirect(offsets)
+                if t < share:
+                    v(vec.tensor_copy(out, win))
+                else:
+                    c(act.activation(out, win, AF.Copy))
+        elif step[0] == "codes":
+            j, n = step[1:]
+            vec.wait_ge(sem.v, vn[0])
+            vec.wait_ge(sem.c, cn[0])
+            s = slice(H * j, H * (j + n))
+            codes[j] = v(vec.quantize_mx(T.qc[:, s], T.qp[:, s], T.e[:, 4 * H * j:4 * H * (j + n)]))
+        else:
+            n = step[1]
+            vec.wait_ge(sem["w%d" % n], 32)
+            a, b = WC * n, WB * (n % 4)
+            packed[n] = v(vec.quantize_mx(T.wc[:, a:a + WC], T.wp[:, a:a + WC], T.wz[:, b:b + WB]))
+
+    for n in range(8):
+        if n == 0:
+            syn.wait_ge(sem.v, zero[0])
+            syn.dma_start(T.wz[:, WB:2 * WB], T.wz[:, 0:WB]).then_inc(sem.ldz, 16)
+            syn.wait_ge(sem.ldz, 16)
+        if n == 2:
+            syn.wait_ge(sem.c, copied)
+        if n >= 2:
+            syn.wait_ge(sem.v, zero[n] if n < 4 else packed[n - 4])
+        b = WB * (n % 4)
+        for p, d in enumerate(sets[n // 2]):
+            a, l = 64 * p + 16 * (2 * pos + n % 2), T.rank_of(d)
+            syn.dma_start(T.wz[a:a + 16, b:b + WB], T.w[16 * l:16 * l + 16, :]).then_inc(sem["w%d" % n], 16)
+
+    def factors(j, owners):
+        for d in owners:
+            l, p = T.rank_of(d), tiles[j].index(d)
             g.iota(T.mul[64 * p:64 * p + 64, 2 * C * j:2 * C * j + 2 * C], [[B[l] - A[l], 2], [0, C]], A[l], 0).then_inc(sem.ix, 1)
 
-    def addresses(j):
-        w, n = slice(4 * C * j, 4 * C * j + 4 * C), slice(2 * C * j, 2 * C * j + 2 * C)
-        for i in (2 * j, 2 * j + 1):
-            for p, d in enumerate(tiles[i]):
-                r = slice(64 * p, 64 * p + 64)
-                m = v(vec.tensor_scalar(T.s1[r, 2 * C * i:2 * C * i + 2 * C], T.xy[r, :], SH[T.rank_of(d)], None,
-                                        Op.arith_shift_right))
-        vec.wait_ge(sem.v, m)
-        vec.wait_ge(sem.v, v(vec.tensor_tensor(T.s2[:, w], T.s1[:, w], T.mul[:, w], Op.mult)))
-        for i in (2 * j, 2 * j + 1):
-            a = 2 * C * i
-            m = v(vec.tensor_tensor(T.s3[:, C * i:C * i + C], T.s2[:, a:a + C], T.s2[:, a + C:a + 2 * C], Op.add))
-        vec.wait_ge(sem.v, m)
-        vec.wait_ge(sem.v, v(vec.tensor_scalar(T.s4[:, n], T.s3[:, n], K - 1, None, Op.bitwise_and)))
-        return v(vec.tensor_copy(T.lst[:, n], T.s4[:, n]))
-
-    for p in range(2):
-        a = 64 * p + 32 - 32 * pos
-        v(vec.memset(T.xy[a:a + 32, :], 0))
-    v(vec.memset(T.offn[dead, :], 0))
-    z0 = v(vec.memset(T.wz[:, 0:WB], 0.0))
-    vec.wait_ge(sem.v, z0)
-    vec.wait_ge(sem.ldl, 128)
-    vec.wait_ge(sem.ix, 8)
-    afar = addresses(0)
-    anear = addresses(1)
-    z2 = v(vec.memset(T.wz[:, 2 * WB:4 * WB], 0.0))
-
-    act.wait_ge(sem.v, z0)
-    z1 = c(act.activation(T.wz[:, WB:2 * WB], T.wz[:, 0:WB], AF.Copy))
-    act.wait_ge(sem.ldt, 80)
-    for t in range(4):
-        apart = c(act.activation(T.tbd[:, K * t:K * t + K], T.tbs[:, t:4 * K:4], AF.Copy))
-    act.wait_ge(sem.c, apart)
-
-    def pick(j):
-        if j:
-            own, other = (slice(64 * pos + 32 * p, 64 * pos + 32 * p + 32) for p in (pos, 1 - pos))
-            vec.wait_ge(sem.v, anear)
-            v(vec.tensor_copy(T.offn[own, 0:C], T.lst[own, 2 * C:3 * C]))
-            vec.wait_ge(sem.ln, 16)
-            a, b = 2 * C * pos, 2 * C * (1 - pos)
-            v(vec.tensor_copy(T.offn[own, C:2 * C], T.nl[own, a + C:a + 2 * C]))
-            m = v(vec.tensor_copy(T.offn[other, :], T.nl[other, b:b + 2 * C]))
-            vec.wait_ge(sem.v, m)
-            act.wait_ge(sem.v, m)
-            vec.wait_ge(sem.c, apart)
-        else:
-            vec.wait_ge(sem.lf, 16)
-            act.wait_ge(sem.lf, 16)
-        a = 8 * H * j
-        for t in range(4):
-            out, win = T.e[:, a + t:a + 8 * H:4], T.tbd[:, K * t:K * t + K].indirect((T.offn if j else T.offf)[:])
-            if t < 2:
-                mv = v(vec.tensor_copy(out, win))
-            else:
-                mc = c(act.activation(out, win, AF.Copy))
-        vec.wait_ge(sem.v, mv)
-        vec.wait_ge(sem.c, mc)
-        s = slice(2 * H * j, 2 * H * j + 2 * H)
-        return v(vec.quantize_mx(T.qc[:, s], T.qp[:, s], T.e[:, a:a + 8 * H]))
-
-    def pack(i):
-        vec.wait_ge(sem["w%d" % i], 64)
-        for h in range(2):
-            a, b = WC * (2 * i + h), WB * (2 * (i % 2) + h)
-            m = v(vec.quantize_mx(T.wc[:, a:a + WC], T.wp[:, a:a + WC], T.wz[:, b:b + WB]))
-        return m
-
-    qnear = pick(1)
-    qfar = pick(0)
-    qw = [pack(i) for i in range(4)]
-
-    for i in range(4):
-        if i:
-            syn.wait_ge(sem.v, z2 if i == 1 else qw[i - 2])
-        else:
-            syn.wait_ge(sem.c, z1)
-        for h in range(2):
-            b = WB * (2 * (i % 2) + h)
-            for p, d in enumerate(sets[i]):
-                a, l = 64 * p + 16 * (2 * pos + h), T.rank_of(d)
-                syn.dma_start(T.wz[a:a + 16, b:b + WB], T.w[16 * l:16 * l + 16, :]).then_inc(sem["w%d" % i], 16)
-
-    g.wait_ge(sem.v, afar)
+    factors(FAR0, tiles[FAR0])
+    factors(FAR1, tiles[FAR1])
+    factors(TWIN, twin)
+    factors(HOME, [core])
+    g.wait_ge(sem.v, blank)
+    g.wait_ge(sem.ldl, 64)
+    g.remote_dma_fused([xfer(topo, core, [mate], every, sem.lm, T.xy[:], T.xm[:])], local_sem=sem.loc)
+    g.wait_ge(sem.v, lists[FAR0])
     both = zip(hs, helpers(topo, mate, ranks))
     g.remote_dma_fused([xfer(topo, core, list(d), e, sem.hl, T.lst[:, C * i:C * i + C], T.hl[:, C * pos:C * pos + C])
                         for i, (d, e) in enumerate(zip(both, (off, rest)))], local_sem=sem.loc)
-    g.wait_ge(sem.v, anear)
-    a = 2 * C * pos
-    g.remote_dma_fused([xfer(topo, core, [d], e, sem.ln, T.lst[:, C * j:C * j + C], T.nl[:, a + C * (j - 2):a + C * (j - 1)])
-                        for d, j, e in ((first, 3, off[:4]), (second, 3, off[4:]), (mate, 2, rest))], local_sem=sem.loc)
-    total = 32
-    s, mysem = slice(H * me, H * me + H), sem["t%d" % me]
+    g.remote_dma_fused([xfer(topo, core, [d], e, sem.ln, T.lst[:, C * TWIN:C * TWIN + C], T.nl[:, C * pos:C * pos + C])
+                        for d, e in ((first, off[:4]), (second, off[4:]))], local_sem=sem.loc)
+    total = 40
+    mine, mysem = slice(H * me, H * me + H), sem["t%d" % me]
 
     def send(ways, helper=False):
         g.remote_dma_fused([xfer(topo, core, [d], e, sem.hcs if helper else mysem, T.qc[:, H * j:H * j + H].bitcast(dt.uint8),
-                                 (T.hc[:] if helper else T.lc[:, s]).bitcast(dt.uint8)) for d, j, e in ways], local_sem=sem.loc)
+                                 (T.hc[:] if helper else T.lc[:, mine]).bitcast(dt.uint8)) for d, j, e in ways], local_sem=sem.loc)
         g.remote_dma_fused([xfer(topo, core, [d], e, sem.hps if helper else mysem, T.qp[:, H * j:H * j + H],
-                                 T.hp[:] if helper else T.lp[:, s]) for d, j, e in ways], local_sem=sem.loc)
+                                 T.hp[:] if helper else T.lp[:, mine]) for d, j, e in ways], local_sem=sem.loc)
         return 2 * sum(len(e) for _, _, e in ways)
 
-    g.wait_ge(sem.v, qnear)
-    total += send([(first, 3, off), (mate, 2, rest)])
-    g.wait_ge(sem.v, qfar)
-    total += send([(hs[0], 0, off), (hs[1], 1, rest)], True)
+    g.wait_ge(sem.v, codes[TWIN])
+    total += send([(first, TWIN, off), (mate, HOME, rest)])
+    for j in (FAR0, FAR1):
+        g.wait_ge(sem.v, codes[j])
+        total += send([(hs[j], j, every)], True)
     early = [d for p in fars for d in p if topo.die(d) == topo.die(core)]
     late = [d for p in fars for d in p if d not in early]
-    every = off + rest
     for d in [first] + early:
         k = slot(topo, d, ranks)
         s, to = slice(H * k, H * k + H), sem["t%d" % k]
@@ -260,26 +279,26 @@ def rank_program(g, core, T, topo):
     g.wait_ge(sem.loc, total)
 
     steps = [core, mate, first, second] + early + late
-    seen = qnear
+    blocks = [(o, h) for o in range(O) for h in range(2)]
+    seen = codes[TWIN]
     pe.wait_ge(sem.v, seen)
     for d in steps:
         i = [j for j, p in enumerate(sets) if d in p][0]
-        if qw[i] > seen:
-            seen = qw[i]
-            pe.wait_ge(sem.v, seen)
         k = slot(topo, d, ranks)
         if d in early:
             pe.wait_ge(sem["u%d" % k], 8)
         if d != core:
             pe.wait_ge(sem["t%d" % k], 8 if d in early else 24 if d in late else 32 if d == second else 16)
-        co, sc = (T.qc[:, 2 * H:3 * H], T.qp[:, 2 * H:3 * H]) if d == core else \
+        co, sc = (T.qc[:, H * HOME:H * HOME + H], T.qp[:, H * HOME:H * HOME + H]) if d == core else \
             (T.lc[:, H * k:H * k + H], T.lp[:, H * k:H * k + H])
-        for o in range(O):
-            for h in range(2):
-                a, b = WC * (2 * i + h) + 128 * o, 512 * (2 * o + h)
-                x = pe.matmul_mx(T.ps[:, b:b + H], T.wc[:, a:a + 128], T.wp[:, a:a + 128], co, sc, d == core, d == steps[-1])
-                if d == steps[-1]:
-                    x.then_inc(sem.m, 1)
+        for o, h in blocks if d == steps[-1] else sorted(blocks, key=lambda x: x[1]):
+            if packed[2 * i + h] > seen:
+                seen = packed[2 * i + h]
+                pe.wait_ge(sem.v, seen)
+            a, b = WC * (2 * i + h) + 128 * o, 512 * (2 * o + h)
+            x = pe.matmul_mx(T.ps[:, b:b + H], T.wc[:, a:a + 128], T.wp[:, a:a + 128], co, sc, d == core, d == steps[-1])
+            if d == steps[-1]:
+                x.then_inc(sem.m, 1)
 
     for o in range(O):
         a, b = TOK * o, 512 * 2 * o

from concourse.bass import DstId, RemoteDMATransfer
from concourse.mybir import dt, AluOpType, ActivationFunctionType

K, TOK, O, G = 256, 256, 3, 8
SH = (7, 6, 5, 4, 3, 2, 1, 0)
A = (1531, 797, 1877, 1129, 619, 1993, 1367, 911)
B = (1013, 1741, 587, 1459, 1907, 733, 1229, 1667)
H = TOK // 2
C = H // 16
WB = 512 * O
WC = 128 * O
FAR0, FAR1, TWIN, HOME = range(4)

PLAN = ([("lists", FAR0, 3), ("zero", 2), ("zero", 3), ("home",), ("pick", HOME, 2), ("pick", TWIN, 2),
         ("codes", TWIN, 2), ("pick", FAR0, 2), ("codes", FAR0, 1), ("pick", FAR1, 2), ("codes", FAR1, 1)]
        + [("pack", n) for n in range(8)])

SCRATCH = {
    "xy": ("sbuf", [128, 2 * C], "int32"), "xm": ("sbuf", [128, 2 * C], "int32"), "mul": ("sbuf", [128, 8 * C], "int32"),
    "s1": ("sbuf", [128, 8 * C], "int32"), "s2": ("sbuf", [128, 8 * C], "int32"),
    "s3": ("sbuf", [128, 4 * C], "int32"), "s4": ("sbuf", [128, 4 * C], "int32"),
    "lst": ("sbuf", [128, 4 * C], "uint16"), "hl": ("sbuf", [128, 2 * C], "uint16"), "nl": ("sbuf", [128, 2 * C], "uint16"),
    "offf": ("sbuf", [128, 2 * C], "uint16"), "offn": ("sbuf", [128, 2 * C], "uint16"),
    "tbs": ("sbuf", [128, 4 * K], "bfloat16"), "tbd": ("sbuf", [128, 4 * K], "bfloat16"),
    "e": ("sbuf", [128, 16 * H], "bfloat16"),
    "qc": ("sbuf", [128, 4 * H], "float8_e4m3fn_x4"), "qp": ("sbuf", [128, 4 * H], "uint8"),
    "wz": ("sbuf", [128, 4 * WB], "bfloat16"),
    "wc": ("sbuf", [128, 8 * WC], "float8_e4m3fn_x4"), "wp": ("sbuf", [128, 8 * WC], "uint8"),
    "hc": ("sbuf", [128, H], "float8_e4m3fn_x4"), "hp": ("sbuf", [128, H], "uint8"),
    "lc": ("sbuf", [128, G * H], "float8_e4m3fn_x4"), "lp": ("sbuf", [128, G * H], "uint8"),
    "acc": ("sbuf", [128, O * TOK], "float32"),
    "ps": ("psum", [128, 512 * 2 * O], "float32"),
}
SEMAPHORES = (["ldl", "ldt", "ldd", "ldz", "lm", "ln", "lf0", "lf1", "ix", "hl", "hcs", "hps", "v", "c", "m", "loc", "sty"]
              + ["w%d" % s for s in range(8)] + ["t%d" % q for q in range(G)] + ["u%d" % q for q in range(G)])


def bits(engines):
    return sum(1 << e for e in engines)


def chips_of(topo, ranks):
    out = []
    for c in ranks:
        if not any(c in p for p in out):
            out.append([d for d in ranks if d in topo.cores_of(c)])
    return out


def far_chips(topo, src, ranks):
    f = [p for p in chips_of(topo, ranks) if not topo.may_write(src, p[0])]
    return sorted(f, key=lambda p: topo.host(p[0]) != topo.host(src))


def helpers(topo, src, ranks):
    f = far_chips(topo, src, ranks)
    return [c for c in topo.cores_of(src) if c not in ranks and topo.die(c) == topo.die(src)
            and all(topo.may_write(c, p[0]) for p in f)][:len(f)]


def slot(topo, core, ranks):
    return [d for p in chips_of(topo, ranks) for d in p].index(core)


def xfer(topo, core, dsts, engines, sem, src, out):
    ids = []
    for d in dsts:
        rid, pid = topo.addr(d, core)
        ids.append(DstId(rid=rid, pnc=pid))
    fold = isinstance(src, list)
    return RemoteDMATransfer(dst_ids=ids, dma_engine_mask=bits(engines), remote_sem=sem, srcs=src if fold else [src],
                             dsts=[out for _ in dsts], alu_op=1 if fold else 0)


def helper_program(g, core, T, topo, ranks):
    for src in ranks:
        hs = helpers(topo, src, ranks)
        if core not in hs:
            continue
        pair = far_chips(topo, src, ranks)[hs.index(core)]
        pair = sorted(pair, key=lambda d: topo.die(d) != topo.die(core))
        eng = topo.engines(core, pair[0])
        k = slot(topo, src, ranks)
        sem, s = T.sem["t%d" % k], slice(H * k, H * k + H)
        j = [src in p for p in far_chips(topo, pair[0], ranks)].index(True)
        g.wait_ge(T.sem.hl, 16)
        g.remote_dma_fused([xfer(topo, core, pair[:1], eng, T.sem["lf%d" % j], [T.hl[:, 0:C], T.hl[:, C:2 * C]],
                                 T.offf[:, C * j:C * j + C])], local_sem=T.sem.loc)
        g.wait_ge(T.sem.hcs, 16)
        g.remote_dma_fused([xfer(topo, core, pair[:1], eng, T.sem["u%d" % k], T.hc[:].bitcast(dt.uint8),
                                 T.lc[:, s].bitcast(dt.uint8))], local_sem=T.sem.loc)
        g.wait_ge(T.sem.hps, 16)
        g.remote_dma_fused([xfer(topo, core, pair, eng, sem, T.hp[:], T.lp[:, s])], local_sem=T.sem.loc)
        g.wait_ge(T.sem.loc, 3 * len(eng))


def rank_program(g, core, T, topo):
    ranks = list(T.cores)
    rank = T.rank_of(core)
    if rank is None:
        helper_program(g, core, T, topo, ranks)
        return
    Op, AF = AluOpType, ActivationFunctionType
    sem, vec, act, pe, syn = T.sem, g.vector, g.scalar, g.tensor, g.sync

    chips = chips_of(topo, ranks)
    fars = far_chips(topo, core, ranks)
    home = [p for p in chips if core in p][0]
    twin = [p for p in chips if p is not home and p not in fars][0]
    tiles = fars + [twin, home]
    sets = [home, twin] + fars
    pos = home.index(core)
    mate = home[1 - pos]
    first, second = sorted(twin, key=lambda d: topo.die(d) != topo.die(core))
    hs = helpers(topo, core, ranks)
    me = slot(topo, core, ranks)
    off = topo.engines(core, first)
    rest = [e for e in topo.engines(core, mate) if e not in off]
    every = off + rest
    live, dead = slice(64 * pos, 64 * pos + 64), slice(64 - 64 * pos, 128 - 64 * pos)
    own, other = (slice(64 * pos + 32 * p, 64 * pos + 32 * p + 32) for p in (pos, 1 - pos))

    for t, (q, name) in enumerate(((syn, "px"), (act, "py"))):
        for h in range(2):
            a = 32 * pos + 16 * h
            q.dma_start(T.xy[a:a + 16, C * t:C * t + C], T[name][:, C * h:C * h + C]).then_inc(sem.ldl, 16)
    for k in range(4):
        a = 64 * pos + 16 * k
        syn.dma_start(T.tbs[a:a + 16, :], T.tb[16 * rank:16 * rank + 16, :]).then_inc(sem.ldt, 16)
    z = 64 if rank < G // 2 else 0
    syn.dma_start(T.tbd[dead, :], T.tb[z:z + 64, :]).then_inc(sem.ldd, 16)

    vn, cn = [0], [0]

    def v(inst):
        inst.then_inc(sem.v, 1)
        vn[0] += 1
        return vn[0]

    def c(inst):
        inst.then_inc(sem.c, 1)
        cn[0] += 1
        return cn[0]

    def addresses(j, n, parts, r, out):
        w, u = slice(2 * C * j, 2 * C * (j + n)), slice(C * j, C * (j + n))
        for i, rows, xy, d in parts:
            m = v(vec.tensor_scalar(T.s1[rows, 2 * C * i:2 * C * i + 2 * C], xy, SH[T.rank_of(d)], None, Op.arith_shift_right))
        vec.wait_ge(sem.ix, 7 if j == HOME else 2 * (j + n))
        vec.wait_ge(sem.v, m)
        vec.wait_ge(sem.v, v(vec.tensor_tensor(T.s2[r, w], T.s1[r, w], T.mul[r, w], Op.mult)))
        for i in range(j, j + n):
            a = 2 * C * i
            m = v(vec.tensor_tensor(T.s3[r, C * i:C * i + C], T.s2[r, a:a + C], T.s2[r, a + C:a + 2 * C], Op.add))
        vec.wait_ge(sem.v, m)
        vec.wait_ge(sem.v, v(vec.tensor_scalar(T.s4[r, u], T.s3[r, u], K - 1, None, Op.bitwise_and)))
        return v(vec.tensor_copy(out, T.s4[r, u]))

    half = WB // 2
    v(vec.memset(T.xy[32 - 32 * pos:64 - 32 * pos, :], 0))
    blank = v(vec.memset(T.xy[64:128, :], 0))
    v(vec.memset(T.offn[dead, :], 0))
    zero = {0: v(vec.memset(T.wz[:, 0:WB], 0.0))}
    seed = v(vec.memset(T.wz[:, 2 * WB:2 * WB + half], 0.0))
    vec.wait_ge(sem.v, zero[0])
    vec.wait_ge(sem.ldl, 64)

    act.wait_ge(sem.ldt, 64)
    for t in range(4):
        apart = c(act.activation(T.tbd[live, K * t:K * t + K], T.tbs[live, t:4 * K:4], AF.Copy))
    act.wait_ge(sem.v, seed)
    copied = c(act.activation(T.wz[:, 3 * WB:3 * WB + half], T.wz[:, 2 * WB:2 * WB + half], AF.Copy))
    act.wait_ge(sem.c, apart)
    act.wait_ge(sem.ldd, 16)

    lists, codes, packed = {}, {}, {}
    for step in PLAN:
        if step[0] == "lists":
            j, n = step[1:]
            parts = [(i, slice(64 * p, 64 * p + 64), T.xy[0:64, :], d) for i in range(j, j + n) for p, d in enumerate(tiles[i])]
            lists[j] = addresses(j, n, parts, slice(0, 128), T.lst[:, C * j:C * (j + n)])
        elif step[0] == "zero":
            n = step[1]
            zero[n] = v(vec.memset(T.wz[:, WB * n + half:WB * n + WB], 0.0))
        elif step[0] == "home":
            vec.wait_ge(sem.lm, 16)
            lists[HOME] = addresses(HOME, 1, [(HOME, own, T.xy[32 * pos:32 * pos + 32, :], core),
                                              (HOME, other, T.xm[32 - 32 * pos:64 - 32 * pos, :], core)],
                                    live, T.offn[live, C:2 * C])
            vec.wait_ge(sem.c, apart)
            vec.wait_ge(sem.ldd, 16)
        elif step[0] == "pick":
            j, share = step[1:]
            if j == TWIN:
                vec.wait_ge(sem.ln, 8)
                for r, p in ((own, pos), (other, 1 - pos)):
                    m = v(vec.tensor_copy(T.offn[r, 0:C], T.nl[r, C * p:C * p + C]))
            for q in (vec, act):
                if j < TWIN:
                    q.wait_ge(sem["lf%d" % j], 8)
                else:
                    q.wait_ge(sem.v, m if j == TWIN else lists[HOME])
            offsets = T.offf[:, C * j:C * j + C] if j < TWIN else T.offn[:, C * (j - TWIN):C * (j - TWIN) + C]
            for t in range(4):
                out, win = T.e[:, 4 * H * j + t:4 * H * (j + 1):4], T.tbd[:, K * t:K * t + K].indirect(offsets)
                if t < share:
                    v(vec.tensor_copy(out, win))
                else:
                    c(act.activation(out, win, AF.Copy))
        elif step[0] == "codes":
            j, n = step[1:]
            vec.wait_ge(sem.v, vn[0])
            vec.wait_ge(sem.c, cn[0])
            s = slice(H * j, H * (j + n))
            codes[j] = v(vec.quantize_mx(T.qc[:, s], T.qp[:, s], T.e[:, 4 * H * j:4 * H * (j + n)]))
        else:
            n = step[1]
            vec.wait_ge(sem["w%d" % n], 32)
            a, b = WC * n, WB * (n % 4)
            packed[n] = v(vec.quantize_mx(T.wc[:, a:a + WC], T.wp[:, a:a + WC], T.wz[:, b:b + WB]))

    for n in range(8):
        if n == 0:
            syn.wait_ge(sem.v, zero[0])
            syn.dma_start(T.wz[:, WB:2 * WB], T.wz[:, 0:WB]).then_inc(sem.ldz, 16)
            syn.wait_ge(sem.ldz, 16)
        if n == 2:
            syn.wait_ge(sem.c, copied)
        if n >= 2:
            syn.wait_ge(sem.v, zero[n] if n < 4 else packed[n - 4])
        b = WB * (n % 4)
        for p, d in enumerate(sets[n // 2]):
            a, l = 64 * p + 16 * (2 * pos + n % 2), T.rank_of(d)
            syn.dma_start(T.wz[a:a + 16, b:b + WB], T.w[16 * l:16 * l + 16, :]).then_inc(sem["w%d" % n], 16)

    def factors(j, owners):
        for d in owners:
            l, p = T.rank_of(d), tiles[j].index(d)
            g.iota(T.mul[64 * p:64 * p + 64, 2 * C * j:2 * C * j + 2 * C], [[B[l] - A[l], 2], [0, C]], A[l], 0).then_inc(sem.ix, 1)

    factors(FAR0, tiles[FAR0])
    factors(FAR1, tiles[FAR1])
    factors(TWIN, twin)
    factors(HOME, [core])
    g.wait_ge(sem.v, blank)
    g.wait_ge(sem.ldl, 64)
    g.remote_dma_fused([xfer(topo, core, [mate], every, sem.lm, T.xy[:], T.xm[:])], local_sem=sem.loc)
    g.wait_ge(sem.v, lists[FAR0])
    both = zip(hs, helpers(topo, mate, ranks))
    g.remote_dma_fused([xfer(topo, core, list(d), e, sem.hl, T.lst[:, C * i:C * i + C], T.hl[:, C * pos:C * pos + C])
                        for i, (d, e) in enumerate(zip(both, (off, rest)))], local_sem=sem.loc)
    g.remote_dma_fused([xfer(topo, core, [d], e, sem.ln, T.lst[:, C * TWIN:C * TWIN + C], T.nl[:, C * pos:C * pos + C])
                        for d, e in ((first, off[:4]), (second, off[4:]))], local_sem=sem.loc)
    total = 40
    mine, mysem = slice(H * me, H * me + H), sem["t%d" % me]

    def send(ways, helper=False):
        g.remote_dma_fused([xfer(topo, core, [d], e, sem.hcs if helper else mysem, T.qc[:, H * j:H * j + H].bitcast(dt.uint8),
                                 (T.hc[:] if helper else T.lc[:, mine]).bitcast(dt.uint8)) for d, j, e in ways], local_sem=sem.loc)
        g.remote_dma_fused([xfer(topo, core, [d], e, sem.hps if helper else mysem, T.qp[:, H * j:H * j + H],
                                 T.hp[:] if helper else T.lp[:, mine]) for d, j, e in ways], local_sem=sem.loc)
        return 2 * sum(len(e) for _, _, e in ways)

    g.wait_ge(sem.v, codes[TWIN])
    total += send([(first, TWIN, off), (mate, HOME, rest)])
    for j in (FAR0, FAR1):
        g.wait_ge(sem.v, codes[j])
        total += send([(hs[j], j, every)], True)
    early = [d for p in fars for d in p if topo.die(d) == topo.die(core)]
    late = [d for p in fars for d in p if d not in early]
    for d in [first] + early:
        k = slot(topo, d, ranks)
        s, to = slice(H * k, H * k + H), sem["t%d" % k]
        g.wait_ge(to if d == first else sem["u%d" % k], 16 if d == first else 8)
        views = [T.lc[:, s].bitcast(dt.uint8)] + ([T.lp[:, s]] if d == first else [])
        for x in views:
            g.remote_dma_fused([xfer(topo, core, [mate], every, to, x, x)], local_sem=sem.loc)
            total += len(every)
    g.wait_ge(sem.loc, total)

    steps = [core, mate, first, second] + early + late
    blocks = [(o, h) for o in range(O) for h in range(2)]
    seen = codes[TWIN]
    pe.wait_ge(sem.v, seen)
    for d in steps:
        i = [j for j, p in enumerate(sets) if d in p][0]
        k = slot(topo, d, ranks)
        if d in early:
            pe.wait_ge(sem["u%d" % k], 8)
        if d != core:
            pe.wait_ge(sem["t%d" % k], 8 if d in early else 24 if d in late else 32 if d == second else 16)
        co, sc = (T.qc[:, H * HOME:H * HOME + H], T.qp[:, H * HOME:H * HOME + H]) if d == core else \
            (T.lc[:, H * k:H * k + H], T.lp[:, H * k:H * k + H])
        for o, h in blocks if d == steps[-1] else sorted(blocks, key=lambda x: x[1]):
            if packed[2 * i + h] > seen:
                seen = packed[2 * i + h]
                pe.wait_ge(sem.v, seen)
            a, b = WC * (2 * i + h) + 128 * o, 512 * (2 * o + h)
            x = pe.matmul_mx(T.ps[:, b:b + H], T.wc[:, a:a + 128], T.wp[:, a:a + 128], co, sc, d == core, d == steps[-1])
            if d == steps[-1]:
                x.then_inc(sem.m, 1)

    for o in range(O):
        a, b = TOK * o, 512 * 2 * o
        vec.wait_ge(sem.m, 2 * o + 1)
        mv = v(vec.tensor_copy(T.acc[:, a:a + H], T.ps[:, b:b + H]))
        act.wait_ge(sem.m, 2 * o + 2)
        mc = c(act.activation(T.acc[:, a + H:a + TOK], T.ps[:, b + 512:b + 512 + H], AF.Copy))
        syn.wait_ge(sem.v, mv)
        syn.wait_ge(sem.c, mc)
        syn.dma_start(T.y[:, a:a + TOK], T.acc[:, a:a + TOK]).then_inc(sem.sty, 16)
    syn.wait_ge(sem.sty, 16 * O)
